import numpy as np
import ml_dtypes


def mxq(x, axis, fmt="e4m3"):
    dtype, down = {"e4m3": (ml_dtypes.float8_e4m3fn, 7), "e5m2": (ml_dtypes.float8_e5m2, 14)}[fmt]
    v = np.moveaxis(np.asarray(x, np.float32).astype(ml_dtypes.bfloat16).astype(np.float64), axis, -1)
    blocks = v.reshape(v.shape[:-1] + (-1, 32))
    amax = np.abs(blocks).max(-1, keepdims=True)
    byte = np.maximum(np.where(amax > 0, np.frexp(amax)[1] - 1 + 127, 0) - down, 1)
    scale = np.exp2(byte - 127.0)
    codes = (blocks / scale).astype(np.float32).astype(dtype).astype(np.float64)
    return np.moveaxis((codes * scale).reshape(v.shape), -1, axis)


WIDE = False


def mx_kscale(k):
    if not WIDE:
        return np.ones(k)
    levels = np.array([10, -10, 5, -5, 0])
    if k % 512:
        return np.exp2(np.random.permutation(np.resize(levels, k // 32))).repeat(32)
    a = np.empty((k // 512, 16))
    for p in range(k // 512):
        a[p, :8] = np.random.permutation(np.resize(levels, 8))
        for g in range(8):
            far = levels[np.abs(levels - a[p, g]) >= 10]
            a[p, g + 8] = far[np.random.randint(len(far))]
    return np.exp2(a.ravel()).repeat(32)


BF16 = ml_dtypes.bfloat16


def bf(x):
    return np.asarray(x, np.float32).astype(BF16)


def f64(x):
    return np.asarray(x).astype(np.float64)


E2M1 = np.array([0.0, 0.5, 1.0, 1.5, 2.0, 3.0, 4.0, 6.0, -0.0, -0.5, -1.0, -1.5, -2.0, -3.0, -4.0, -6.0])


def pack_weight(w, fmt):
    k, n = w.shape
    w = f64(bf(w)).reshape(k // 32, 32, n)
    amax = np.abs(w).max(1)
    if fmt == "e4m3":
        byte = np.frexp(amax)[1] - 1 + 127 - 7
    else:
        mant, ex = np.frexp(amax / 6.0)
        byte = np.where(mant > 0.5, ex, ex - 1) + 127
    byte = np.clip(np.where(amax > 0, byte, 1), 1, 254)
    scaled = (w * np.exp2(127.0 - byte)[:, None, :]).reshape(k, n).astype(np.float32)
    by_word = np.ascontiguousarray(scaled.reshape(k // 512, 128, 4, n).transpose(0, 1, 3, 2))
    if fmt == "e4m3":
        words = by_word.astype(ml_dtypes.float8_e4m3fn).view(np.uint8)
    else:
        c = by_word.astype(ml_dtypes.float4_e2m1fn).view(np.uint8) & 0xF
        words = c[..., 0::2] | (c[..., 1::2] << 4)
    return np.ascontiguousarray(words), np.ascontiguousarray(byte.astype(np.uint8).reshape(k // 512, 16, n))


def unpack_weight(words, scales, fmt):
    g, p, n, _ = words.shape
    if fmt == "e4m3":
        vals = np.ascontiguousarray(words).view(ml_dtypes.float8_e4m3fn).astype(np.float64)
    else:
        nib = np.empty((g, p, n, 4), np.uint8)
        nib[..., 0::2] = words & 0xF
        nib[..., 1::2] = words >> 4
        vals = E2M1[nib]
    vals = vals * np.repeat(np.exp2(scales.astype(np.float64) - 127.0), 8, axis=1)[..., None]
    return vals.transpose(0, 1, 3, 2).reshape(g * 512, n)
def pack4(w):
    words, scales = pack_weight(w, "e2m1")
    return words.reshape(words.shape[0], 128, -1), scales


def unpack4(words, scales):
    return unpack_weight(words.reshape(words.shape[0], 128, -1, 2), scales, "e2m1")


M, T, F = 2048, 1024, 1024


def setup_inputs():
    s = mx_kscale(T)
    u = mx_kscale(M)
    dev = 0.6 * np.random.standard_normal((M, T))
    cross = 0.8 * np.random.standard_normal((T, T)) / np.sqrt(T)
    elast = cross - 0.4 * np.eye(T)
    base = np.exp(0.3 * np.random.standard_normal((M, T)))
    ptdf = np.random.standard_normal((M, F)) / np.sqrt(M)
    words, scales = pack4(ptdf / u[:, None])
    return {"dev": bf(dev * s),
            "elast": bf(elast / s[:, None]),
            "shift": bf(0.3 * np.random.standard_normal(T)),
            "base": bf(base * u[:, None]),
            "ptdf_words": words,
            "ptdf_scales": scales}


def reference(dev, elast, shift, base, ptdf_words, ptdf_scales):
    y = mxq(f64(dev), 1, "e4m3") @ mxq(f64(elast), 0, "e4m3")
    load = f64(base) * np.exp(y + f64(shift))
    w = unpack4(ptdf_words, ptdf_scales)
    flow = w.T @ mxq(load, 0, "e4m3")
    return flow

@@ -1,0 +1,346 @@
+from contextlib import ExitStack
+
+import concourse.mybir as mybir
+from concourse.masks import make_identity
+
+NODES, PERIODS, LINES = 2048, 1024, 1024
+FLOPS = 2 * NODES * PERIODS * PERIODS + 2 * NODES * LINES * PERIODS
+
+F32 = mybir.dt.float32
+BF16 = mybir.dt.bfloat16
+U32 = mybir.dt.uint32
+I32 = mybir.dt.int32
+U8 = mybir.dt.uint8
+FP8X4 = mybir.dt.float8_e4m3fn_x4
+FP4X4 = mybir.dt.float4_e2m1fn_x4
+ADD = mybir.AluOpType.add
+MULT = mybir.AluOpType.mult
+EXP = mybir.ActivationFunctionType.Exp
+
+P = 128
+PACK = 4
+K_PASS = P * PACK
+BANK = 512
+GROUPS = NODES // K_PASS
+J_PASSES = PERIODS // K_PASS
+HALVES = PERIODS // BANK
+LINE_TILES = LINES // P
+UNITS = HALVES * GROUPS
+RUN = 2
+COPY_RUN = 4
+Y_BANKS = (0, 1, 2)
+TURN_BANKS = (3, 4)
+
+
+def tile_cross_period_demand_flows_s13_kernel(tc, dev, elast, shift, base, ptdf_words, ptdf_scales, out):
+    nc = tc.nc
+    with ExitStack() as ctx:
+        keep = ctx.enter_context(tc.tile_pool(name="keep", bufs=1))
+        work = ctx.enter_context(tc.tile_pool(name="work", bufs=3))
+        psum = ctx.enter_context(tc.psum_pool(name="psum", bufs=1))
+        ctx.enter_context(tc.manual_schedule())
+
+        def bank(b, name):
+            return psum.tile([P, BANK], F32, name=name, tag="bank%d" % b)
+
+        dev_rows = dev.rearrange("(g p t) j -> g p t j", p=P, t=PACK)
+        base_rows = base.rearrange("(g p t) h -> g p t h", p=P, t=PACK)
+        elast_rows = elast.rearrange("(c p t) h -> c p t h", p=P, t=PACK)
+
+        dev_raw, elast_raw, base_raw = {}, {}, {}
+
+        def load_dev(g, t0, t1):
+            raw = keep.tile([P, t1 - t0, PERIODS], BF16, name="dev_%d_%d" % (g, t0))
+            nc.sync.dma_start(out=raw[:], in_=dev_rows[g, :, t0:t1, :])
+            for t in range(t0, t1):
+                dev_raw[g, t] = raw[:, t - t0, :]
+
+        def load_elast(c, half):
+            raw = keep.tile([P, PACK, BANK], BF16, name="elast_%d_%d" % (c, half))
+            nc.sync.dma_start(out=raw[:], in_=elast_rows[c, :, :, half * BANK : (half + 1) * BANK])
+            elast_raw[c, half] = raw
+
+        def load_base(unit):
+            half, g = divmod(unit, GROUPS)
+            raw = keep.tile([P, PACK, BANK], BF16, name="base_%d" % unit)
+            nc.sync.dma_start(out=raw[:], in_=base_rows[g, :, :, half * BANK : (half + 1) * BANK])
+            base_raw[unit] = raw
+
+        w_codes = {}
+        w_scales = keep.tile([P, GROUPS, LINES], U8, name="w_scales", align_bytes=64)
+
+        def load_w_codes(g0, g1):
+            codes = keep.tile([P, g1 - g0, 2 * LINES], U8, name="w_codes_%d" % g0, align_bytes=64)
+            nc.sync.dma_start(out=codes[:].bitcast(I32), in_=ptdf_words[g0:g1].rearrange("g p n -> p g n").bitcast(I32))
+            for g in range(g0, g1):
+                w_codes[g] = codes[:, g - g0, :]
+
+        def load_w_scales():
+            for q in range(4):
+                nc.sync.dma_start(
+                    out=w_scales[32 * q : 32 * q + 4].bitcast(I32),
+                    in_=ptdf_scales[:, 4 * q : 4 * q + 4, :].rearrange("g r n -> r g n").bitcast(I32),
+                )
+
+        ident = keep.tile([P, P], F32, name="ident")
+        make_identity(nc, ident[:])
+        per_part = PERIODS // P
+        shift_raw = keep.tile([P, per_part], BF16, name="shift_raw")
+        nc.scalar.dma_start(out=shift_raw[:], in_=shift.rearrange("(p c) -> p c", p=P))
+        nc.vector.memset(w_scales[:].rearrange("p g n -> p (g n)").bitcast(I32), 0)
+        warm = keep.tile([P, 1], F32, name="warm")
+        nc.scalar.activation(out=warm[:], in_=ident[:, 0:1], func=EXP)
+
+        load_dev(0, 0, 1)
+        load_elast(0, 0)
+        load_dev(0, 1, 2)
+        load_elast(1, 0)
+        load_dev(0, 2, 4)
+        load_dev(1, 0, 2)
+        load_base(0)
+        load_dev(1, 2, 4)
+        load_dev(2, 0, 4)
+        load_elast(0, 1)
+        load_base(1)
+        load_w_scales()
+        load_w_codes(0, 2)
+        load_dev(3, 0, 4)
+        load_elast(1, 1)
+        load_base(2)
+        load_w_codes(2, 4)
+        for unit in range(3, UNITS):
+            load_base(unit)
+
+        shift_cols = keep.tile([P, per_part], F32, name="shift_cols")
+        shift_all = keep.tile([P, PERIODS], F32, name="shift_all")
+
+        def spread_shift():
+            nc.vector.tensor_copy(out=shift_cols[:], in_=shift_raw[:])
+            for part in range(2):
+                spread = bank(Y_BANKS[part], "spread_%d" % part)
+                for c in range(4):
+                    col = 4 * part + c
+                    nc.tensor.transpose(
+                        spread[:, c * P : (c + 1) * P], shift_cols[:, col : col + 1].to_broadcast([P, P]), ident[:]
+                    )
+                nc.scalar.copy(
+                    out=shift_all[:].rearrange("p (k c) -> p k c", c=per_part)[:, :, 4 * part : 4 * part + 4],
+                    in_=spread[:].rearrange("p (c k) -> p k c", c=4),
+                )
+
+        elast_grouped, elast_q = {}, {}
+
+        def group_elast(copy, c, half, h0, h1):
+            if (c, half) not in elast_grouped:
+                elast_grouped[c, half] = work.tile(
+                    [P, BANK, PACK], BF16, name="eg_%d_%d" % (c, half), tag="eg", bufs=2, align_bytes=64
+                )
+            copy(
+                out=elast_grouped[c, half][:, h0:h1, :].rearrange("p (c i) t -> p c t i", i=COPY_RUN),
+                in_=elast_raw[c, half][:, :, h0:h1].rearrange("p t (c i) -> p c t i", i=COPY_RUN),
+            )
+
+        def quantize(name, grouped, width):
+            codes = keep.tile([P, width], U32, name=name + "_codes", align_bytes=64)
+            scales = keep.tile([P, width], U8, name=name + "_scales", align_bytes=64)
+            nc.vector.quantize_mx(out=codes[:].bitcast(FP8X4), scales=scales[:], in_=grouped)
+            return codes, scales
+
+        def quantize_elast(c, half):
+            elast_q[c, half] = quantize(
+                "eq_%d_%d" % (c, half), elast_grouped[c, half][:].rearrange("p h t -> p (h t)"), BANK
+            )
+
+        dev_grouped, dev_q = {}, {}
+
+        def turn_dev(g, t):
+            pair, slot = divmod(t, 2)
+            if slot == 0:
+                dev_grouped[g, pair] = work.tile(
+                    [P, 2, J_PASSES, P * PACK], BF16, name="dg_%d_%d" % (g, pair), tag="dg", align_bytes=64
+                )
+            words = dev_raw[g, t].bitcast(F32)
+            turned = bank(TURN_BANKS[slot], "turned_%d_%d" % (g, t))
+            for c in range(J_PASSES):
+                for u in range(2):
+                    nc.tensor.transpose(
+                        turned[:, (2 * c + u) * P : (2 * c + u + 1) * P],
+                        words[:, 256 * c + u : 256 * (c + 1) : 2],
+                        ident[:],
+                    )
+            nc.scalar.copy(
+                out=dev_grouped[g, pair][:, slot].bitcast(F32).rearrange("p c (n u) -> p c n u", u=2),
+                in_=turned[:].rearrange("p (c u n) -> p c n u", c=J_PASSES, u=2),
+            )
+
+        def quantize_dev(g, pair):
+            dev_q[g, pair] = quantize(
+                "dq_%d_%d" % (g, pair), dev_grouped[g, pair][:].rearrange("p s c n -> p (s c n)"), 2 * J_PASSES * P
+            )
+
+        response, sums = {}, {}
+
+        def respond(unit, t):
+            half, g = divmod(unit, GROUPS)
+            pair, slot = divmod(t, 2)
+            y = bank(Y_BANKS[(PACK * unit + t + 2) % len(Y_BANKS)], "y_%d_%d" % (unit, t))
+            d_codes, d_scales = dev_q[g, pair]
+            for c in range(J_PASSES):
+                cols = slice((J_PASSES * slot + c) * P, (J_PASSES * slot + c + 1) * P)
+                e_codes, e_scales = elast_q[c, half]
+                nc.tensor.matmul_mx(
+                    out=y[:],
+                    lhsT=d_codes[:, cols].bitcast(FP8X4),
+                    lhsT_scale=d_scales[:, cols],
+                    rhs=e_codes[:].bitcast(FP8X4),
+                    rhs_scale=e_scales[:],
+                    start=(c == 0),
+                    stop=(c == J_PASSES - 1),
+                )
+            sums[unit, t] = y
+
+        def add_shift(unit, t):
+            half = unit // GROUPS
+            y = sums[unit, t]
+            if t == 0:
+                response[unit] = work.tile([P, PACK, BANK], F32, name="resp_%d" % unit, tag="resp")
+            nc.vector.tensor_tensor(
+                out=response[unit][:, t, :], in0=y[:], in1=shift_all[:, half * BANK : (half + 1) * BANK], op=ADD
+            )
+
+        def exponentiate(unit, t0, t1):
+            part = response[unit][:, t0:t1, :]
+            nc.scalar.activation(out=part, in_=part, func=EXP)
+
+        load_grouped, load_q = {}, {}
+
+        def scale_base(unit):
+            load_grouped[unit] = work.tile([P, BANK, PACK], BF16, name="lg_%d" % unit, tag="lg", bufs=2, align_bytes=64)
+            nc.vector.tensor_tensor(
+                out=load_grouped[unit][:].rearrange("p (c i) t -> p c t i", i=RUN),
+                in0=response[unit][:].rearrange("p t (c i) -> p c t i", i=RUN),
+                in1=base_raw[unit][:].rearrange("p t (c i) -> p c t i", i=RUN),
+                op=MULT,
+            )
+
+        def quantize_load(unit):
+            load_q[unit] = quantize("lq_%d" % unit, load_grouped[unit][:].rearrange("p h t -> p (h t)"), BANK)
+
+        flows = {}
+
+        def flow_pass(half, f, g, b=None):
+            if g == 0:
+                flows[half, f] = bank(b, "flow_%d_%d" % (half, f))
+            l_codes, l_scales = load_q[half * GROUPS + g]
+            nc.tensor.matmul_mx(
+                out=flows[half, f][:],
+                lhsT=w_codes[g][:, 2 * P * f : 2 * P * (f + 1)].bitcast(FP4X4),
+                lhsT_scale=w_scales[:, g, P * f : P * (f + 1)],
+                rhs=l_codes[:].bitcast(FP8X4),
+                rhs_scale=l_scales[:],
+                start=(g == 0),
+                stop=(g == GROUPS - 1),
+            )
+
+        def store_flow(copy, half, f):
+            done = work.tile([P, BANK], F32, name="done_%d_%d" % (half, f), tag="done", bufs=LINE_TILES)
+            copy(out=done[:], in_=flows[half, f][:])
+            nc.sync.dma_start(out=out[P * f : P * (f + 1), half * BANK : (half + 1) * BANK], in_=done[:])
+
+        on_act, on_vec = nc.scalar.copy, nc.vector.tensor_copy
+        free_banks = (5, 6, 7) + TURN_BANKS
+
+        spread_shift()
+        turn_dev(0, 0)
+        group_elast(on_vec, 0, 0, 0, BANK)
+        turn_dev(0, 1)
+        quantize_elast(0, 0)
+        group_elast(on_vec, 1, 0, 0, BANK)
+        quantize_dev(0, 0)
+        turn_dev(0, 2)
+        turn_dev(0, 3)
+        quantize_elast(1, 0)
+
+        last = UNITS - 1
+
+        def passes(half, lines, groups, banks=None):
+            for n, f in enumerate(lines):
+                for g in groups:
+                    flow_pass(half, f, g, banks[n] if g == 0 else None)
+
+        early = {
+            2: [(0, range(3), [0], free_banks)],
+            3: [(0, range(3), [1], None), (0, range(3, 5), [0, 1], free_banks[3:])],
+            5: [(0, [5], range(GROUPS), free_banks[0:])],
+            6: [(0, [7], range(GROUPS), free_banks[2:])],
+        }
+        late = {
+            3: [(0, range(5), [2], None)],
+            4: [(0, range(5), [3], None)],
+            5: [(0, [6], range(GROUPS), free_banks[1:])],
+            6: [(1, range(2), [0, 1], free_banks[3:])],
+        }
+        stores_mid = {5: [2, 3, 4], 6: [6, 7]}
+        stores_end = {4: [0, 1], 5: [5]}
+
+        respond(0, 0)
+        respond(0, 1)
+        for unit in range(last):
+            ahead = unit + 1
+            add_shift(unit, 0)
+            if unit < GROUPS:
+                quantize_dev(unit, 1)
+            add_shift(unit, 1)
+            for job in early.get(unit, []):
+                passes(*job)
+            if ahead < GROUPS:
+                turn_dev(ahead, 0)
+                turn_dev(ahead, 1)
+            exponentiate(unit, 0, 2)
+            for f in stores_mid.get(unit, []):
+                store_flow(on_act, 0, f)
+            if 0 < unit < GROUPS - 1:
+                group_elast(on_act, unit - 1, 1, 0, BANK // 2)
+            if unit > 0:
+                scale_base(unit - 1)
+            if ahead < GROUPS:
+                quantize_dev(ahead, 0)
+            if unit == GROUPS - 1:
+                quantize_elast(1, 1)
+            respond(unit, 2)
+            respond(unit, 3)
+            add_shift(unit, 2)
+            if unit > 0:
+                quantize_load(unit - 1)
+            add_shift(unit, 3)
+            if ahead < GROUPS:
+                turn_dev(ahead, 2)
+                turn_dev(ahead, 3)
+            respond(ahead, 0)
+            respond(ahead, 1)
+            for job in late.get(unit, []):
+                passes(*job)
+            exponentiate(unit, 2, 4)
+            for f in stores_end.get(unit, []):
+                store_flow(on_act, 0, f)
+            if 0 < unit < GROUPS - 1:
+                group_elast(on_act, unit - 1, 1, BANK // 2, BANK)
+            if unit == GROUPS - 2:
+                quantize_elast(0, 1)
+
+        for t in range(PACK):
+            if t > 1:
+                respond(last, t)
+            add_shift(last, t)
+            if t % 2 == 1:
+                exponentiate(last, t - 1, t + 1)
+        passes(1, range(2, 5), [0, 1], free_banks)
+        passes(1, range(5, 8), [0, 1], [Y_BANKS[(PACK * last + t + 2) % len(Y_BANKS)] for t in range(1, PACK)])
+        scale_base(last - 1)
+        quantize_load(last - 1)
+        passes(1, range(LINE_TILES), [2])
+        scale_base(last)
+        quantize_load(last)
+        for f in range(LINE_TILES):
+            flow_pass(1, f, 3)
+            store_flow(on_vec if f % 2 == 0 else on_act, 1, f)

@@ -26,8 +26,9 @@ J_PASSES = PERIODS // K_PASS
 HALVES = PERIODS // BANK
 LINE_TILES = LINES // P
 UNITS = HALVES * GROUPS
-RUN = 2
+RUN = 4
 COPY_RUN = 4
+HEAD_SPLIT = 352
 Y_BANKS = (0, 1, 2)
 TURN_BANKS = (3, 4)
 
@@ -82,18 +83,30 @@ def tile_cross_period_demand_flows_s13_kernel(tc, dev, elast, shift, base, ptdf_
                     in_=ptdf_scales[:, 4 * q : 4 * q + 4, :].rearrange("g r n -> r g n").bitcast(I32),
                 )
 
+        def mx_tiles(name, width):
+            codes = keep.tile([P, width], U32, name=name + "_codes", align_bytes=64)
+            scales = keep.tile([P, width], U8, name=name + "_scales", align_bytes=64)
+            return codes, scales
+
+        def quantize(name, grouped, width):
+            codes, scales = mx_tiles(name, width)
+            nc.vector.quantize_mx(out=codes[:].bitcast(FP8X4), scales=scales[:], in_=grouped)
+            return codes, scales
+
         ident = keep.tile([P, P], F32, name="ident")
         make_identity(nc, ident[:])
         per_part = PERIODS // P
         shift_raw = keep.tile([P, per_part], BF16, name="shift_raw")
         nc.scalar.dma_start(out=shift_raw[:], in_=shift.rearrange("(p c) -> p c", p=P))
+        ones = keep.tile([P, PACK * BANK], BF16, name="ones", align_bytes=64)
+        nc.vector.memset(ones[:].bitcast(I32), 0)
+        warm_codes, warm_scales = quantize("warm", ones[:], BANK)
         nc.vector.memset(w_scales[:].rearrange("p g n -> p (g n)").bitcast(I32), 0)
         warm = keep.tile([P, 1], F32, name="warm")
         nc.scalar.activation(out=warm[:], in_=ident[:, 0:1], func=EXP)
 
-        load_dev(0, 0, 1)
         load_elast(0, 0)
-        load_dev(0, 1, 2)
+        load_dev(0, 0, 2)
         load_elast(1, 0)
         load_dev(0, 2, 4)
         load_dev(1, 0, 2)
@@ -111,22 +124,17 @@ def tile_cross_period_demand_flows_s13_kernel(tc, dev, elast, shift, base, ptdf_
         for unit in range(3, UNITS):
             load_base(unit)
 
-        shift_cols = keep.tile([P, per_part], F32, name="shift_cols")
-        shift_all = keep.tile([P, PERIODS], F32, name="shift_all")
+        shift_all = keep.tile([P, PERIODS], BF16, name="shift_all")
 
         def spread_shift():
-            nc.vector.tensor_copy(out=shift_cols[:], in_=shift_raw[:])
-            for part in range(2):
-                spread = bank(Y_BANKS[part], "spread_%d" % part)
-                for c in range(4):
-                    col = 4 * part + c
-                    nc.tensor.transpose(
-                        spread[:, c * P : (c + 1) * P], shift_cols[:, col : col + 1].to_broadcast([P, P]), ident[:]
-                    )
-                nc.scalar.copy(
-                    out=shift_all[:].rearrange("p (k c) -> p k c", c=per_part)[:, :, 4 * part : 4 * part + 4],
-                    in_=spread[:].rearrange("p (c k) -> p k c", c=4),
-                )
+            pairs = shift_raw[:].bitcast(F32)
+            spread = bank(Y_BANKS[0], "spread")
+            for c in range(per_part // 2):
+                nc.tensor.transpose(spread[:, c * P : (c + 1) * P], pairs[:, c : c + 1].to_broadcast([P, P]), ident[:])
+            nc.scalar.copy(
+                out=shift_all[:].bitcast(F32).rearrange("p (k c) -> p k c", c=per_part // 2),
+                in_=spread[:].rearrange("p (c k) -> p k c", c=per_part // 2),
+            )
 
         elast_grouped, elast_q = {}, {}
 
@@ -139,12 +147,6 @@ def tile_cross_period_demand_flows_s13_kernel(tc, dev, elast, shift, base, ptdf_
                 out=elast_grouped[c, half][:, h0:h1, :].rearrange("p (c i) t -> p c t i", i=COPY_RUN),
                 in_=elast_raw[c, half][:, :, h0:h1].rearrange("p t (c i) -> p c t i", i=COPY_RUN),
             )
-
-        def quantize(name, grouped, width):
-            codes = keep.tile([P, width], U32, name=name + "_codes", align_bytes=64)
-            scales = keep.tile([P, width], U8, name=name + "_scales", align_bytes=64)
-            nc.vector.quantize_mx(out=codes[:].bitcast(FP8X4), scales=scales[:], in_=grouped)
-            return codes, scales
 
         def quantize_elast(c, half):
             elast_q[c, half] = quantize(
@@ -214,17 +216,27 @@ def tile_cross_period_demand_flows_s13_kernel(tc, dev, elast, shift, base, ptdf_
 
         load_grouped, load_q = {}, {}
 
-        def scale_base(unit):
-            load_grouped[unit] = work.tile([P, BANK, PACK], BF16, name="lg_%d" % unit, tag="lg", bufs=2, align_bytes=64)
+        def scale_base(unit, h0=0, h1=BANK):
+            if h0 == 0:
+                load_grouped[unit] = work.tile(
+                    [P, BANK, PACK], BF16, name="lg_%d" % unit, tag="lg", bufs=2, align_bytes=64
+                )
             nc.vector.tensor_tensor(
-                out=load_grouped[unit][:].rearrange("p (c i) t -> p c t i", i=RUN),
-                in0=response[unit][:].rearrange("p t (c i) -> p c t i", i=RUN),
-                in1=base_raw[unit][:].rearrange("p t (c i) -> p c t i", i=RUN),
+                out=load_grouped[unit][:, h0:h1, :].rearrange("p (c i) t -> p c t i", i=RUN),
+                in0=response[unit][:, :, h0:h1].rearrange("p t (c i) -> p c t i", i=RUN),
+                in1=base_raw[unit][:, :, h0:h1].rearrange("p t (c i) -> p c t i", i=RUN),
                 op=MULT,
             )
 
-        def quantize_load(unit):
-            load_q[unit] = quantize("lq_%d" % unit, load_grouped[unit][:].rearrange("p h t -> p (h t)"), BANK)
+        def quantize_load(unit, h0=0, h1=BANK):
+            if h0 == 0:
+                load_q[unit] = mx_tiles("lq_%d" % unit, BANK)
+            codes, scales = load_q[unit]
+            nc.vector.quantize_mx(
+                out=codes[:, h0:h1].bitcast(FP8X4),
+                scales=scales[:, h0:h1],
+                in_=load_grouped[unit][:, h0:h1, :].rearrange("p h t -> p (h t)"),
+            )
 
         flows = {}
 
@@ -247,19 +259,37 @@ def tile_cross_period_demand_flows_s13_kernel(tc, dev, elast, shift, base, ptdf_
             copy(out=done[:], in_=flows[half, f][:])
             nc.sync.dma_start(out=out[P * f : P * (f + 1), half * BANK : (half + 1) * BANK], in_=done[:])
 
+        idle = bank(7, "idle")
+
+        def keep_warm(count):
+            for n in range(count):
+                nc.tensor.matmul_mx(
+                    out=idle[:],
+                    lhsT=warm_codes[:, :P].bitcast(FP8X4),
+                    lhsT_scale=warm_scales[:, :P],
+                    rhs=warm_codes[:].bitcast(FP8X4),
+                    rhs_scale=warm_scales[:],
+                    start=True,
+                    stop=True,
+                )
+
         on_act, on_vec = nc.scalar.copy, nc.vector.tensor_copy
         free_banks = (5, 6, 7) + TURN_BANKS
 
+        keep_warm(2)
         spread_shift()
+        keep_warm(2)
+        group_elast(on_act, 0, 0, HEAD_SPLIT, BANK)
+        group_elast(on_vec, 0, 0, 0, HEAD_SPLIT)
         turn_dev(0, 0)
-        group_elast(on_vec, 0, 0, 0, BANK)
         turn_dev(0, 1)
+        keep_warm(3)
         quantize_elast(0, 0)
         group_elast(on_vec, 1, 0, 0, BANK)
         quantize_dev(0, 0)
+        quantize_elast(1, 0)
         turn_dev(0, 2)
         turn_dev(0, 3)
-        quantize_elast(1, 0)
 
         last = UNITS - 1
 
@@ -336,11 +366,12 @@ def tile_cross_period_demand_flows_s13_kernel(tc, dev, elast, shift, base, ptdf_
                 exponentiate(last, t - 1, t + 1)
         passes(1, range(2, 5), [0, 1], free_banks)
         passes(1, range(5, 8), [0, 1], [Y_BANKS[(PACK * last + t + 2) % len(Y_BANKS)] for t in range(1, PACK)])
-        scale_base(last - 1)
-        quantize_load(last - 1)
-        passes(1, range(LINE_TILES), [2])
-        scale_base(last)
-        quantize_load(last)
+        for unit in (last - 1, last):
+            for step in (scale_base, quantize_load):
+                step(unit, 0, BANK // 2)
+                step(unit, BANK // 2, BANK)
+            if unit < last:
+                passes(1, range(LINE_TILES), [2])
         for f in range(LINE_TILES):
             flow_pass(1, f, 3)
             store_flow(on_vec if f % 2 == 0 else on_act, 1, f)

@@ -29,6 +29,7 @@ UNITS = HALVES * GROUPS
 RUN = 4
 COPY_RUN = 4
 HEAD_SPLIT = 352
+POOL_SHARE = 192
 Y_BANKS = (0, 1, 2)
 TURN_BANKS = (3, 4)
 
@@ -83,24 +84,11 @@ def tile_cross_period_demand_flows_s13_kernel(tc, dev, elast, shift, base, ptdf_
                     in_=ptdf_scales[:, 4 * q : 4 * q + 4, :].rearrange("g r n -> r g n").bitcast(I32),
                 )
 
-        def mx_tiles(name, width):
-            codes = keep.tile([P, width], U32, name=name + "_codes", align_bytes=64)
-            scales = keep.tile([P, width], U8, name=name + "_scales", align_bytes=64)
-            return codes, scales
-
-        def quantize(name, grouped, width):
-            codes, scales = mx_tiles(name, width)
-            nc.vector.quantize_mx(out=codes[:].bitcast(FP8X4), scales=scales[:], in_=grouped)
-            return codes, scales
-
         ident = keep.tile([P, P], F32, name="ident")
         make_identity(nc, ident[:])
         per_part = PERIODS // P
         shift_raw = keep.tile([P, per_part], BF16, name="shift_raw")
         nc.scalar.dma_start(out=shift_raw[:], in_=shift.rearrange("(p c) -> p c", p=P))
-        ones = keep.tile([P, PACK * BANK], BF16, name="ones", align_bytes=64)
-        nc.vector.memset(ones[:].bitcast(I32), 0)
-        warm_codes, warm_scales = quantize("warm", ones[:], BANK)
         nc.vector.memset(w_scales[:].rearrange("p g n -> p (g n)").bitcast(I32), 0)
         warm = keep.tile([P, 1], F32, name="warm")
         nc.scalar.activation(out=warm[:], in_=ident[:, 0:1], func=EXP)
@@ -147,6 +135,16 @@ def tile_cross_period_demand_flows_s13_kernel(tc, dev, elast, shift, base, ptdf_
                 out=elast_grouped[c, half][:, h0:h1, :].rearrange("p (c i) t -> p c t i", i=COPY_RUN),
                 in_=elast_raw[c, half][:, :, h0:h1].rearrange("p t (c i) -> p c t i", i=COPY_RUN),
             )
+
+        def mx_tiles(name, width):
+            codes = keep.tile([P, width], U32, name=name + "_codes", align_bytes=64)
+            scales = keep.tile([P, width], U8, name=name + "_scales", align_bytes=64)
+            return codes, scales
+
+        def quantize(name, grouped, width):
+            codes, scales = mx_tiles(name, width)
+            nc.vector.quantize_mx(out=codes[:].bitcast(FP8X4), scales=scales[:], in_=grouped)
+            return codes, scales
 
         def quantize_elast(c, half):
             elast_q[c, half] = quantize(
@@ -216,11 +214,21 @@ def tile_cross_period_demand_flows_s13_kernel(tc, dev, elast, shift, base, ptdf_
 
         load_grouped, load_q = {}, {}
 
+        def new_load_tile(unit):
+            load_grouped[unit] = work.tile([P, BANK, PACK], BF16, name="lg_%d" % unit, tag="lg", bufs=1, align_bytes=64)
+
+        def scale_base_on_pool(unit):
+            new_load_tile(unit)
+            nc.gpsimd.tensor_tensor(
+                out=load_grouped[unit][:, :POOL_SHARE, :],
+                in0=response[unit][:, :, :POOL_SHARE].rearrange("p t h -> p h t"),
+                in1=base_raw[unit][:, :, :POOL_SHARE].rearrange("p t h -> p h t"),
+                op=MULT,
+            )
+
         def scale_base(unit, h0=0, h1=BANK):
-            if h0 == 0:
-                load_grouped[unit] = work.tile(
-                    [P, BANK, PACK], BF16, name="lg_%d" % unit, tag="lg", bufs=2, align_bytes=64
-                )
+            if unit not in load_grouped:
+                new_load_tile(unit)
             nc.vector.tensor_tensor(
                 out=load_grouped[unit][:, h0:h1, :].rearrange("p (c i) t -> p c t i", i=RUN),
                 in0=response[unit][:, :, h0:h1].rearrange("p t (c i) -> p c t i", i=RUN),
@@ -229,7 +237,7 @@ def tile_cross_period_demand_flows_s13_kernel(tc, dev, elast, shift, base, ptdf_
             )
 
         def quantize_load(unit, h0=0, h1=BANK):
-            if h0 == 0:
+            if unit not in load_q:
                 load_q[unit] = mx_tiles("lq_%d" % unit, BANK)
             codes, scales = load_q[unit]
             nc.vector.quantize_mx(
@@ -259,31 +267,14 @@ def tile_cross_period_demand_flows_s13_kernel(tc, dev, elast, shift, base, ptdf_
             copy(out=done[:], in_=flows[half, f][:])
             nc.sync.dma_start(out=out[P * f : P * (f + 1), half * BANK : (half + 1) * BANK], in_=done[:])
 
-        idle = bank(7, "idle")
-
-        def keep_warm(count):
-            for n in range(count):
-                nc.tensor.matmul_mx(
-                    out=idle[:],
-                    lhsT=warm_codes[:, :P].bitcast(FP8X4),
-                    lhsT_scale=warm_scales[:, :P],
-                    rhs=warm_codes[:].bitcast(FP8X4),
-                    rhs_scale=warm_scales[:],
-                    start=True,
-                    stop=True,
-                )
-
         on_act, on_vec = nc.scalar.copy, nc.vector.tensor_copy
         free_banks = (5, 6, 7) + TURN_BANKS
 
-        keep_warm(2)
         spread_shift()
-        keep_warm(2)
         group_elast(on_act, 0, 0, HEAD_SPLIT, BANK)
         group_elast(on_vec, 0, 0, 0, HEAD_SPLIT)
         turn_dev(0, 0)
         turn_dev(0, 1)
-        keep_warm(3)
         quantize_elast(0, 0)
         group_elast(on_vec, 1, 0, 0, BANK)
         quantize_dev(0, 0)
@@ -298,80 +289,100 @@ def tile_cross_period_demand_flows_s13_kernel(tc, dev, elast, shift, base, ptdf_
                 for g in groups:
                     flow_pass(half, f, g, banks[n] if g == 0 else None)
 
-        early = {
+        second = {
             2: [(0, range(3), [0], free_banks)],
             3: [(0, range(3), [1], None), (0, range(3, 5), [0, 1], free_banks[3:])],
-            5: [(0, [5], range(GROUPS), free_banks[0:])],
-            6: [(0, [7], range(GROUPS), free_banks[2:])],
+            4: [(0, range(5), [2], None)],
+            5: [(0, range(5), [3], None)],
+            6: [(0, [6, 7], range(GROUPS), free_banks[1:])],
+            7: [(1, range(2), [1], None), (1, range(2, 5), [0, 1], free_banks)],
         }
-        late = {
-            3: [(0, range(5), [2], None)],
-            4: [(0, range(5), [3], None)],
-            5: [(0, [6], range(GROUPS), free_banks[1:])],
-            6: [(1, range(2), [0, 1], free_banks[3:])],
+        second_late = {
+            5: [(0, [5], range(GROUPS), free_banks)],
+            6: [(1, range(2), [0], free_banks[3:])],
         }
-        stores_mid = {5: [2, 3, 4], 6: [6, 7]}
-        stores_end = {4: [0, 1], 5: [5]}
+        stores_mid = {5: [0], 6: [3, 4]}
+        stores_end = {5: [1, 2], 6: [5, 6, 7]}
+        half_bank = BANK // 2
 
         respond(0, 0)
         respond(0, 1)
-        for unit in range(last):
+        add_shift(0, 0)
+        quantize_dev(0, 1)
+        add_shift(0, 1)
+        turn_dev(1, 0)
+        turn_dev(1, 1)
+        exponentiate(0, 0, 2)
+        quantize_dev(1, 0)
+        respond(0, 2)
+        respond(0, 3)
+        add_shift(0, 2)
+        add_shift(0, 3)
+        turn_dev(1, 2)
+        turn_dev(1, 3)
+        respond(1, 0)
+        respond(1, 1)
+        exponentiate(0, 2, 4)
+        for unit in range(1, UNITS):
             ahead = unit + 1
+            if unit > 1:
+                scale_base_on_pool(unit - 1)
             add_shift(unit, 0)
-            if unit < GROUPS:
-                quantize_dev(unit, 1)
-            add_shift(unit, 1)
-            for job in early.get(unit, []):
-                passes(*job)
+            if unit == 1:
+                quantize_dev(1, 1)
+                respond(1, 2)
             if ahead < GROUPS:
                 turn_dev(ahead, 0)
                 turn_dev(ahead, 1)
-            exponentiate(unit, 0, 2)
-            for f in stores_mid.get(unit, []):
-                store_flow(on_act, 0, f)
-            if 0 < unit < GROUPS - 1:
-                group_elast(on_act, unit - 1, 1, 0, BANK // 2)
-            if unit > 0:
-                scale_base(unit - 1)
-            if ahead < GROUPS:
-                quantize_dev(ahead, 0)
-            if unit == GROUPS - 1:
-                quantize_elast(1, 1)
-            respond(unit, 2)
             respond(unit, 3)
+            add_shift(unit, 1)
+            if unit == 1:
+                scale_base(0)
+            exponentiate(unit, 0, 2)
             add_shift(unit, 2)
-            if unit > 0:
-                quantize_load(unit - 1)
             add_shift(unit, 3)
             if ahead < GROUPS:
                 turn_dev(ahead, 2)
                 turn_dev(ahead, 3)
-            respond(ahead, 0)
-            respond(ahead, 1)
-            for job in late.get(unit, []):
+                quantize_dev(ahead, 0)
+            for job in second.get(unit, []):
                 passes(*job)
+            for f in stores_mid.get(unit, []):
+                store_flow(on_act, 0, f)
             exponentiate(unit, 2, 4)
             for f in stores_end.get(unit, []):
                 store_flow(on_act, 0, f)
-            if 0 < unit < GROUPS - 1:
-                group_elast(on_act, unit - 1, 1, BANK // 2, BANK)
-            if unit == GROUPS - 2:
+            for job in second_late.get(unit, []):
+                passes(*job)
+            if unit in (1, 2):
+                group_elast(on_act, 0, 1, (unit - 1) * half_bank, unit * half_bank)
+            if unit == 2:
+                group_elast(on_act, 1, 1, 0, BANK)
+            if unit == 3:
                 quantize_elast(0, 1)
+            if 1 < unit < GROUPS:
+                scale_base(unit - 1, POOL_SHARE, BANK)
+            elif unit > 1:
+                scale_base(unit - 1, half_bank, BANK)
+                scale_base(unit - 1, POOL_SHARE, half_bank)
+            if ahead < GROUPS:
+                quantize_dev(ahead, 1)
+            if unit == 3:
+                quantize_elast(1, 1)
+            if ahead < UNITS:
+                for t in range(len(Y_BANKS)):
+                    respond(ahead, t)
+            if unit < GROUPS:
+                quantize_load(unit - 1)
+            else:
+                quantize_load(unit - 1, half_bank, BANK)
+                quantize_load(unit - 1, 0, half_bank)
 
-        for t in range(PACK):
-            if t > 1:
-                respond(last, t)
-            add_shift(last, t)
-            if t % 2 == 1:
-                exponentiate(last, t - 1, t + 1)
-        passes(1, range(2, 5), [0, 1], free_banks)
         passes(1, range(5, 8), [0, 1], [Y_BANKS[(PACK * last + t + 2) % len(Y_BANKS)] for t in range(1, PACK)])
-        for unit in (last - 1, last):
-            for step in (scale_base, quantize_load):
-                step(unit, 0, BANK // 2)
-                step(unit, BANK // 2, BANK)
-            if unit < last:
-                passes(1, range(LINE_TILES), [2])
+        passes(1, range(LINE_TILES), [2])
+        for step in (scale_base, quantize_load):
+            step(last, 0, half_bank)
+            step(last, half_bank, BANK)
         for f in range(LINE_TILES):
             flow_pass(1, f, 3)
             store_flow(on_vec if f % 2 == 0 else on_act, 1, f)

@@ -29,7 +29,8 @@ UNITS = HALVES * GROUPS
 RUN = 4
 COPY_RUN = 4
 HEAD_SPLIT = 352
-POOL_SHARE = 192
+POOL_SHARE = 128
+POOL_RUN = 2
 Y_BANKS = (0, 1, 2)
 TURN_BANKS = (3, 4)
 
@@ -220,9 +221,9 @@ def tile_cross_period_demand_flows_s13_kernel(tc, dev, elast, shift, base, ptdf_
         def scale_base_on_pool(unit):
             new_load_tile(unit)
             nc.gpsimd.tensor_tensor(
-                out=load_grouped[unit][:, :POOL_SHARE, :],
-                in0=response[unit][:, :, :POOL_SHARE].rearrange("p t h -> p h t"),
-                in1=base_raw[unit][:, :, :POOL_SHARE].rearrange("p t h -> p h t"),
+                out=load_grouped[unit][:, :POOL_SHARE, :].rearrange("p (c i) t -> p c t i", i=POOL_RUN),
+                in0=response[unit][:, :, :POOL_SHARE].rearrange("p t (c i) -> p c t i", i=POOL_RUN),
+                in1=base_raw[unit][:, :, :POOL_SHARE].rearrange("p t (c i) -> p c t i", i=POOL_RUN),
                 op=MULT,
             )
 
@@ -294,15 +295,14 @@ def tile_cross_period_demand_flows_s13_kernel(tc, dev, elast, shift, base, ptdf_
             3: [(0, range(3), [1], None), (0, range(3, 5), [0, 1], free_banks[3:])],
             4: [(0, range(5), [2], None)],
             5: [(0, range(5), [3], None)],
-            6: [(0, [6, 7], range(GROUPS), free_banks[1:])],
+            6: [(0, [6, 7], range(GROUPS), free_banks[1:]), (1, [0], [0], free_banks[3:])],
             7: [(1, range(2), [1], None), (1, range(2, 5), [0, 1], free_banks)],
         }
         second_late = {
             5: [(0, [5], range(GROUPS), free_banks)],
-            6: [(1, range(2), [0], free_banks[3:])],
+            6: [(1, [1], [0], free_banks[4:])],
         }
-        stores_mid = {5: [0], 6: [3, 4]}
-        stores_end = {5: [1, 2], 6: [5, 6, 7]}
+        stores_end = {5: range(4), 6: range(4, 8)}
         half_bank = BANK // 2
 
         respond(0, 0)
@@ -323,6 +323,7 @@ def tile_cross_period_demand_flows_s13_kernel(tc, dev, elast, shift, base, ptdf_
         respond(1, 0)
         respond(1, 1)
         exponentiate(0, 2, 4)
+        group_elast(on_act, 0, 1, 0, half_bank)
         for unit in range(1, UNITS):
             ahead = unit + 1
             if unit > 1:
@@ -347,32 +348,29 @@ def tile_cross_period_demand_flows_s13_kernel(tc, dev, elast, shift, base, ptdf_
                 quantize_dev(ahead, 0)
             for job in second.get(unit, []):
                 passes(*job)
-            for f in stores_mid.get(unit, []):
-                store_flow(on_act, 0, f)
             exponentiate(unit, 2, 4)
             for f in stores_end.get(unit, []):
                 store_flow(on_act, 0, f)
-            for job in second_late.get(unit, []):
-                passes(*job)
-            if unit in (1, 2):
-                group_elast(on_act, 0, 1, (unit - 1) * half_bank, unit * half_bank)
+            if unit == 1:
+                group_elast(on_act, 0, 1, half_bank, BANK)
             if unit == 2:
                 group_elast(on_act, 1, 1, 0, BANK)
             if unit == 3:
                 quantize_elast(0, 1)
-            if 1 < unit < GROUPS:
+                quantize_elast(1, 1)
+            if 1 < unit < GROUPS - 1:
                 scale_base(unit - 1, POOL_SHARE, BANK)
             elif unit > 1:
                 scale_base(unit - 1, half_bank, BANK)
                 scale_base(unit - 1, POOL_SHARE, half_bank)
             if ahead < GROUPS:
                 quantize_dev(ahead, 1)
-            if unit == 3:
-                quantize_elast(1, 1)
             if ahead < UNITS:
                 for t in range(len(Y_BANKS)):
                     respond(ahead, t)
-            if unit < GROUPS:
+            for job in second_late.get(unit, []):
+                passes(*job)
+            if unit < GROUPS - 1:
                 quantize_load(unit - 1)
             else:
                 quantize_load(unit - 1, half_bank, BANK)

@@ -21,18 +21,21 @@ P = 128
 PACK = 4
 K_PASS = P * PACK
 BANK = 512
+HALF_BANK = BANK // 2
 GROUPS = NODES // K_PASS
 J_PASSES = PERIODS // K_PASS
-HALVES = PERIODS // BANK
 LINE_TILES = LINES // P
-UNITS = HALVES * GROUPS
+UNITS = (PERIODS // BANK) * GROUPS
+LAST = UNITS - 1
+
 RUN = 4
-COPY_RUN = 4
-HEAD_SPLIT = 352
-POOL_SHARE = 128
 POOL_RUN = 2
+HEAD_SPLIT = 352
+POOL_SHARE = 176
+
 Y_BANKS = (0, 1, 2)
 TURN_BANKS = (3, 4)
+FLOW_BANKS = (5, 6, 7) + TURN_BANKS
 
 
 def tile_cross_period_demand_flows_s13_kernel(tc, dev, elast, shift, base, ptdf_words, ptdf_scales, out):
@@ -46,11 +49,27 @@ def tile_cross_period_demand_flows_s13_kernel(tc, dev, elast, shift, base, ptdf_
         def bank(b, name):
             return psum.tile([P, BANK], F32, name=name, tag="bank%d" % b)
 
+        def y_bank(unit, t):
+            return Y_BANKS[(PACK * unit + t - 1) % len(Y_BANKS)]
+
+        def periods_of(half):
+            return slice(half * BANK, (half + 1) * BANK)
+
+        def in_runs(slots_first, run):
+            return slots_first.rearrange("p t (c i) -> p c t i", i=run)
+
+        def grouped_in_runs(grouped, run):
+            return grouped.rearrange("p (c i) t -> p c t i", i=run)
+
+        def mx_tiles(name, width):
+            codes = keep.tile([P, width], U32, name=name + "_codes", align_bytes=64)
+            scales = keep.tile([P, width], U8, name=name + "_scales", align_bytes=64)
+            return codes, scales
+
         dev_rows = dev.rearrange("(g p t) j -> g p t j", p=P, t=PACK)
         base_rows = base.rearrange("(g p t) h -> g p t h", p=P, t=PACK)
         elast_rows = elast.rearrange("(c p t) h -> c p t h", p=P, t=PACK)
-
-        dev_raw, elast_raw, base_raw = {}, {}, {}
+        dev_raw, elast_raw, base_raw, w_codes = {}, {}, {}, {}
 
         def load_dev(g, t0, t1):
             raw = keep.tile([P, t1 - t0, PERIODS], BF16, name="dev_%d_%d" % (g, t0))
@@ -60,17 +79,14 @@ def tile_cross_period_demand_flows_s13_kernel(tc, dev, elast, shift, base, ptdf_
 
         def load_elast(c, half):
             raw = keep.tile([P, PACK, BANK], BF16, name="elast_%d_%d" % (c, half))
-            nc.sync.dma_start(out=raw[:], in_=elast_rows[c, :, :, half * BANK : (half + 1) * BANK])
+            nc.sync.dma_start(out=raw[:], in_=elast_rows[c, :, :, periods_of(half)])
             elast_raw[c, half] = raw
 
         def load_base(unit):
             half, g = divmod(unit, GROUPS)
             raw = keep.tile([P, PACK, BANK], BF16, name="base_%d" % unit)
-            nc.sync.dma_start(out=raw[:], in_=base_rows[g, :, :, half * BANK : (half + 1) * BANK])
+            nc.sync.dma_start(out=raw[:], in_=base_rows[g, :, :, periods_of(half)])
             base_raw[unit] = raw
-
-        w_codes = {}
-        w_scales = keep.tile([P, GROUPS, LINES], U8, name="w_scales", align_bytes=64)
 
         def load_w_codes(g0, g1):
             codes = keep.tile([P, g1 - g0, 2 * LINES], U8, name="w_codes_%d" % g0, align_bytes=64)
@@ -78,8 +94,10 @@ def tile_cross_period_demand_flows_s13_kernel(tc, dev, elast, shift, base, ptdf_
             for g in range(g0, g1):
                 w_codes[g] = codes[:, g - g0, :]
 
+        w_scales = keep.tile([P, GROUPS, LINES], U8, name="w_scales", align_bytes=64)
+
         def load_w_scales():
-            for q in range(4):
+            for q in range(P // 32):
                 nc.sync.dma_start(
                     out=w_scales[32 * q : 32 * q + 4].bitcast(I32),
                     in_=ptdf_scales[:, 4 * q : 4 * q + 4, :].rearrange("g r n -> r g n").bitcast(I32),
@@ -87,42 +105,41 @@ def tile_cross_period_demand_flows_s13_kernel(tc, dev, elast, shift, base, ptdf_
 
         ident = keep.tile([P, P], F32, name="ident")
         make_identity(nc, ident[:])
-        per_part = PERIODS // P
-        shift_raw = keep.tile([P, per_part], BF16, name="shift_raw")
+        shift_per_part = PERIODS // P
+        shift_raw = keep.tile([P, shift_per_part], BF16, name="shift_raw")
         nc.scalar.dma_start(out=shift_raw[:], in_=shift.rearrange("(p c) -> p c", p=P))
         nc.vector.memset(w_scales[:].rearrange("p g n -> p (g n)").bitcast(I32), 0)
-        warm = keep.tile([P, 1], F32, name="warm")
-        nc.scalar.activation(out=warm[:], in_=ident[:, 0:1], func=EXP)
 
         load_elast(0, 0)
         load_dev(0, 0, 2)
         load_elast(1, 0)
-        load_dev(0, 2, 4)
+        load_dev(0, 2, PACK)
         load_dev(1, 0, 2)
         load_base(0)
-        load_dev(1, 2, 4)
-        load_dev(2, 0, 4)
+        load_dev(1, 2, PACK)
+        load_dev(2, 0, PACK)
         load_elast(0, 1)
         load_base(1)
+        load_dev(3, 0, PACK)
         load_w_scales()
         load_w_codes(0, 2)
-        load_dev(3, 0, 4)
         load_elast(1, 1)
         load_base(2)
-        load_w_codes(2, 4)
-        for unit in range(3, UNITS):
-            load_base(unit)
+        load_w_codes(2, GROUPS)
+        for later_unit in range(3, UNITS):
+            load_base(later_unit)
 
         shift_all = keep.tile([P, PERIODS], BF16, name="shift_all")
 
         def spread_shift():
+            words = shift_per_part // 2
             pairs = shift_raw[:].bitcast(F32)
             spread = bank(Y_BANKS[0], "spread")
-            for c in range(per_part // 2):
+            for c in range(words):
                 nc.tensor.transpose(spread[:, c * P : (c + 1) * P], pairs[:, c : c + 1].to_broadcast([P, P]), ident[:])
             nc.scalar.copy(
-                out=shift_all[:].bitcast(F32).rearrange("p (k c) -> p k c", c=per_part // 2),
-                in_=spread[:].rearrange("p (c k) -> p k c", c=per_part // 2),
+                out=shift_all[:].bitcast(F32).rearrange("p (k c) -> p k c", c=words),
+                in_=spread[:].rearrange("p (c k) -> p k c", c=words),
             )
 
         elast_grouped, elast_q = {}, {}
@@ -130,83 +147,83 @@ def tile_cross_period_demand_flows_s13_kernel(tc, dev, elast, shift, base, ptdf_
         def group_elast(copy, c, half, h0, h1):
             if (c, half) not in elast_grouped:
                 elast_grouped[c, half] = work.tile(
-                    [P, BANK, PACK], BF16, name="eg_%d_%d" % (c, half), tag="eg", bufs=2, align_bytes=64
+                    [P, BANK, PACK], BF16, name="eg_%d_%d" % (c, half), tag="eg", bufs=J_PASSES, align_bytes=64
                 )
             copy(
-                out=elast_grouped[c, half][:, h0:h1, :].rearrange("p (c i) t -> p c t i", i=COPY_RUN),
-                in_=elast_raw[c, half][:, :, h0:h1].rearrange("p t (c i) -> p c t i", i=COPY_RUN),
+                out=grouped_in_runs(elast_grouped[c, half][:, h0:h1, :], RUN),
+                in_=in_runs(elast_raw[c, half][:, :, h0:h1], RUN),
             )
-
-        def mx_tiles(name, width):
-            codes = keep.tile([P, width], U32, name=name + "_codes", align_bytes=64)
-            scales = keep.tile([P, width], U8, name=name + "_scales", align_bytes=64)
-            return codes, scales
-
-        def quantize(name, grouped, width):
-            codes, scales = mx_tiles(name, width)
-            nc.vector.quantize_mx(out=codes[:].bitcast(FP8X4), scales=scales[:], in_=grouped)
-            return codes, scales
 
         def quantize_elast(c, half):
-            elast_q[c, half] = quantize(
-                "eq_%d_%d" % (c, half), elast_grouped[c, half][:].rearrange("p h t -> p (h t)"), BANK
+            codes, scales = mx_tiles("eq_%d_%d" % (c, half), BANK)
+            nc.vector.quantize_mx(
+                out=codes[:].bitcast(FP8X4),
+                scales=scales[:],
+                in_=elast_grouped[c, half][:].rearrange("p h t -> p (h t)"),
             )
+            elast_q[c, half] = codes, scales
 
         dev_grouped, dev_q = {}, {}
 
         def turn_dev(g, t):
-            pair, slot = divmod(t, 2)
-            if slot == 0:
+            pair, member = divmod(t, 2)
+            if member == 0:
                 dev_grouped[g, pair] = work.tile(
                     [P, 2, J_PASSES, P * PACK], BF16, name="dg_%d_%d" % (g, pair), tag="dg", align_bytes=64
                 )
             words = dev_raw[g, t].bitcast(F32)
-            turned = bank(TURN_BANKS[slot], "turned_%d_%d" % (g, t))
+            pass_words = K_PASS // 2
+            turned = bank(TURN_BANKS[member], "turned_%d_%d" % (g, t))
             for c in range(J_PASSES):
                 for u in range(2):
                     nc.tensor.transpose(
                         turned[:, (2 * c + u) * P : (2 * c + u + 1) * P],
-                        words[:, 256 * c + u : 256 * (c + 1) : 2],
+                        words[:, pass_words * c + u : pass_words * (c + 1) : 2],
                         ident[:],
                     )
             nc.scalar.copy(
-                out=dev_grouped[g, pair][:, slot].bitcast(F32).rearrange("p c (n u) -> p c n u", u=2),
+                out=dev_grouped[g, pair][:, member].bitcast(F32).rearrange("p c (n u) -> p c n u", u=2),
                 in_=turned[:].rearrange("p (c u n) -> p c n u", c=J_PASSES, u=2),
             )
 
+        def turn_dev_pair(g, pair):
+            turn_dev(g, 2 * pair)
+            turn_dev(g, 2 * pair + 1)
+
         def quantize_dev(g, pair):
-            dev_q[g, pair] = quantize(
-                "dq_%d_%d" % (g, pair), dev_grouped[g, pair][:].rearrange("p s c n -> p (s c n)"), 2 * J_PASSES * P
+            codes, scales = mx_tiles("dq_%d_%d" % (g, pair), 2 * J_PASSES * P)
+            nc.vector.quantize_mx(
+                out=codes[:].bitcast(FP8X4),
+                scales=scales[:],
+                in_=dev_grouped[g, pair][:].rearrange("p s c n -> p (s c n)"),
             )
+            dev_q[g, pair] = codes, scales
 
-        response, sums = {}, {}
+        y_sums, response = {}, {}
 
-        def respond(unit, t):
+        def first_product(unit, t):
             half, g = divmod(unit, GROUPS)
-            pair, slot = divmod(t, 2)
-            y = bank(Y_BANKS[(PACK * unit + t + 2) % len(Y_BANKS)], "y_%d_%d" % (unit, t))
+            pair, member = divmod(t, 2)
+            y_sums[unit, t] = bank(y_bank(unit, t), "y_%d_%d" % (unit, t))
             d_codes, d_scales = dev_q[g, pair]
             for c in range(J_PASSES):
-                cols = slice((J_PASSES * slot + c) * P, (J_PASSES * slot + c + 1) * P)
+                nodes = slice((J_PASSES * member + c) * P, (J_PASSES * member + c + 1) * P)
                 e_codes, e_scales = elast_q[c, half]
                 nc.tensor.matmul_mx(
-                    out=y[:],
-                    lhsT=d_codes[:, cols].bitcast(FP8X4),
-                    lhsT_scale=d_scales[:, cols],
+                    out=y_sums[unit, t][:],
+                    lhsT=d_codes[:, nodes].bitcast(FP8X4),
+                    lhsT_scale=d_scales[:, nodes],
                     rhs=e_codes[:].bitcast(FP8X4),
                     rhs_scale=e_scales[:],
                     start=(c == 0),
                     stop=(c == J_PASSES - 1),
                 )
-            sums[unit, t] = y
 
         def add_shift(unit, t):
-            half = unit // GROUPS
-            y = sums[unit, t]
             if t == 0:
                 response[unit] = work.tile([P, PACK, BANK], F32, name="resp_%d" % unit, tag="resp")
             nc.vector.tensor_tensor(
-                out=response[unit][:, t, :], in0=y[:], in1=shift_all[:, half * BANK : (half + 1) * BANK], op=ADD
+                out=response[unit][:, t, :], in0=y_sums[unit, t][:], in1=shift_all[:, periods_of(unit // GROUPS)], op=ADD
             )
 
         def exponentiate(unit, t0, t1):
@@ -215,29 +232,19 @@ def tile_cross_period_demand_flows_s13_kernel(tc, dev, elast, shift, base, ptdf_
 
         load_grouped, load_q = {}, {}
 
-        def new_load_tile(unit):
-            load_grouped[unit] = work.tile([P, BANK, PACK], BF16, name="lg_%d" % unit, tag="lg", bufs=1, align_bytes=64)
-
-        def scale_base_on_pool(unit):
-            new_load_tile(unit)
-            nc.gpsimd.tensor_tensor(
-                out=load_grouped[unit][:, :POOL_SHARE, :].rearrange("p (c i) t -> p c t i", i=POOL_RUN),
-                in0=response[unit][:, :, :POOL_SHARE].rearrange("p t (c i) -> p c t i", i=POOL_RUN),
-                in1=base_raw[unit][:, :, :POOL_SHARE].rearrange("p t (c i) -> p c t i", i=POOL_RUN),
-                op=MULT,
-            )
-
-        def scale_base(unit, h0=0, h1=BANK):
+        def scale_base(engine, run, unit, h0, h1):
             if unit not in load_grouped:
-                new_load_tile(unit)
-            nc.vector.tensor_tensor(
-                out=load_grouped[unit][:, h0:h1, :].rearrange("p (c i) t -> p c t i", i=RUN),
-                in0=response[unit][:, :, h0:h1].rearrange("p t (c i) -> p c t i", i=RUN),
-                in1=base_raw[unit][:, :, h0:h1].rearrange("p t (c i) -> p c t i", i=RUN),
+                load_grouped[unit] = work.tile(
+                    [P, BANK, PACK], BF16, name="lg_%d" % unit, tag="lg", bufs=1, align_bytes=64
+                )
+            engine.tensor_tensor(
+                out=grouped_in_runs(load_grouped[unit][:, h0:h1, :], run),
+                in0=in_runs(response[unit][:, :, h0:h1], run),
+                in1=in_runs(base_raw[unit][:, :, h0:h1], run),
                 op=MULT,
             )
 
-        def quantize_load(unit, h0=0, h1=BANK):
+        def quantize_load(unit, h0, h1):
             if unit not in load_q:
                 load_q[unit] = mx_tiles("lq_%d" % unit, BANK)
             codes, scales = load_q[unit]
@@ -249,138 +256,139 @@ def tile_cross_period_demand_flows_s13_kernel(tc, dev, elast, shift, base, ptdf_
 
         flows = {}
 
-        def flow_pass(half, f, g, b=None):
-            if g == 0:
-                flows[half, f] = bank(b, "flow_%d_%d" % (half, f))
-            l_codes, l_scales = load_q[half * GROUPS + g]
-            nc.tensor.matmul_mx(
-                out=flows[half, f][:],
-                lhsT=w_codes[g][:, 2 * P * f : 2 * P * (f + 1)].bitcast(FP4X4),
-                lhsT_scale=w_scales[:, g, P * f : P * (f + 1)],
-                rhs=l_codes[:].bitcast(FP8X4),
-                rhs_scale=l_scales[:],
-                start=(g == 0),
-                stop=(g == GROUPS - 1),
-            )
+        def second_product(half, line_tiles, groups, banks=()):
+            for n, f in enumerate(line_tiles):
+                for g in groups:
+                    if g == 0:
+                        flows[half, f] = bank(banks[n], "flow_%d_%d" % (half, f))
+                    l_codes, l_scales = load_q[half * GROUPS + g]
+                    nc.tensor.matmul_mx(
+                        out=flows[half, f][:],
+                        lhsT=w_codes[g][:, 2 * P * f : 2 * P * (f + 1)].bitcast(FP4X4),
+                        lhsT_scale=w_scales[:, g, P * f : P * (f + 1)],
+                        rhs=l_codes[:].bitcast(FP8X4),
+                        rhs_scale=l_scales[:],
+                        start=(g == 0),
+                        stop=(g == GROUPS - 1),
+                    )
 
         def store_flow(copy, half, f):
             done = work.tile([P, BANK], F32, name="done_%d_%d" % (half, f), tag="done", bufs=LINE_TILES)
             copy(out=done[:], in_=flows[half, f][:])
-            nc.sync.dma_start(out=out[P * f : P * (f + 1), half * BANK : (half + 1) * BANK], in_=done[:])
+            nc.sync.dma_start(out=out[P * f : P * (f + 1), periods_of(half)], in_=done[:])
 
-        on_act, on_vec = nc.scalar.copy, nc.vector.tensor_copy
-        free_banks = (5, 6, 7) + TURN_BANKS
+        on_scalar, on_vector = nc.scalar.copy, nc.vector.tensor_copy
 
         spread_shift()
-        group_elast(on_act, 0, 0, HEAD_SPLIT, BANK)
-        group_elast(on_vec, 0, 0, 0, HEAD_SPLIT)
-        turn_dev(0, 0)
-        turn_dev(0, 1)
+        group_elast(on_scalar, 0, 0, HEAD_SPLIT, BANK)
+        group_elast(on_vector, 0, 0, 0, HEAD_SPLIT)
+        turn_dev_pair(0, 0)
         quantize_elast(0, 0)
-        group_elast(on_vec, 1, 0, 0, BANK)
+        group_elast(on_vector, 1, 0, 0, BANK)
         quantize_dev(0, 0)
         quantize_elast(1, 0)
-        turn_dev(0, 2)
-        turn_dev(0, 3)
+        turn_dev_pair(0, 1)
 
-        last = UNITS - 1
-
-        def passes(half, lines, groups, banks=None):
-            for n, f in enumerate(lines):
-                for g in groups:
-                    flow_pass(half, f, g, banks[n] if g == 0 else None)
-
-        second = {
-            2: [(0, range(3), [0], free_banks)],
-            3: [(0, range(3), [1], None), (0, range(3, 5), [0, 1], free_banks[3:])],
-            4: [(0, range(5), [2], None)],
-            5: [(0, range(5), [3], None)],
-            6: [(0, [6, 7], range(GROUPS), free_banks[1:]), (1, [0], [0], free_banks[3:])],
-            7: [(1, range(2), [1], None), (1, range(2, 5), [0, 1], free_banks)],
-        }
-        second_late = {
-            5: [(0, [5], range(GROUPS), free_banks)],
-            6: [(1, [1], [0], free_banks[4:])],
-        }
-        stores_end = {5: range(4), 6: range(4, 8)}
-        half_bank = BANK // 2
-
-        respond(0, 0)
-        respond(0, 1)
+        first_product(0, 0)
+        first_product(0, 1)
         add_shift(0, 0)
+        exponentiate(0, 0, 1)
         quantize_dev(0, 1)
         add_shift(0, 1)
-        turn_dev(1, 0)
-        turn_dev(1, 1)
-        exponentiate(0, 0, 2)
+        turn_dev_pair(1, 0)
+        exponentiate(0, 1, 2)
         quantize_dev(1, 0)
-        respond(0, 2)
-        respond(0, 3)
+        first_product(0, 2)
+        first_product(0, 3)
         add_shift(0, 2)
         add_shift(0, 3)
-        turn_dev(1, 2)
-        turn_dev(1, 3)
-        respond(1, 0)
-        respond(1, 1)
-        exponentiate(0, 2, 4)
-        group_elast(on_act, 0, 1, 0, half_bank)
-        for unit in range(1, UNITS):
-            ahead = unit + 1
-            if unit > 1:
-                scale_base_on_pool(unit - 1)
+        turn_dev_pair(1, 1)
+        first_product(1, 0)
+        first_product(1, 1)
+        exponentiate(0, 2, PACK)
+        group_elast(on_scalar, 0, 1, 0, HALF_BANK)
+
+        add_shift(1, 0)
+        quantize_dev(1, 1)
+        turn_dev_pair(2, 0)
+        first_product(1, 2)
+        first_product(1, 3)
+        add_shift(1, 1)
+        scale_base(nc.vector, RUN, 0, 0, BANK)
+        quantize_dev(2, 0)
+        exponentiate(1, 0, 2)
+        add_shift(1, 2)
+        add_shift(1, 3)
+        turn_dev_pair(2, 1)
+        exponentiate(1, 2, PACK)
+        group_elast(on_scalar, 0, 1, HALF_BANK, BANK)
+        quantize_dev(2, 1)
+        for t in range(len(Y_BANKS)):
+            first_product(2, t)
+        quantize_load(0, 0, BANK)
+
+        after_unit = {
+            2: [(0, range(3), [0], FLOW_BANKS)],
+            3: [(0, range(3), [1]), (0, range(3, 5), [0, 1], FLOW_BANKS[3:])],
+            4: [(0, range(5), [2])],
+            5: [(0, range(5), [3])],
+            6: [(0, [6, 7], range(GROUPS), FLOW_BANKS[1:]), (1, [0], [0], FLOW_BANKS[3:])],
+            7: [(1, range(2), [1]), (1, range(2, 5), [0, 1], FLOW_BANKS)],
+        }
+        after_next = {
+            5: [(0, [5], range(GROUPS), FLOW_BANKS)],
+            6: [(1, [1], [0], FLOW_BANKS[4:])],
+        }
+        stores = {5: range(4), 6: range(4, LINE_TILES)}
+        last_turn = GROUPS - 2
+        last_of_half = GROUPS - 1
+
+        for unit in range(2, UNITS):
+            before, ahead = unit - 1, unit + 1
+            scale_base(nc.gpsimd, POOL_RUN, before, 0, POOL_SHARE)
             add_shift(unit, 0)
-            if unit == 1:
-                quantize_dev(1, 1)
-                respond(1, 2)
-            if ahead < GROUPS:
-                turn_dev(ahead, 0)
-                turn_dev(ahead, 1)
-            respond(unit, 3)
+            if unit == last_turn:
+                turn_dev_pair(ahead, 0)
+            first_product(unit, PACK - 1)
             add_shift(unit, 1)
-            if unit == 1:
-                scale_base(0)
             exponentiate(unit, 0, 2)
             add_shift(unit, 2)
             add_shift(unit, 3)
-            if ahead < GROUPS:
-                turn_dev(ahead, 2)
-                turn_dev(ahead, 3)
+            if unit == last_turn:
+                turn_dev_pair(ahead, 1)
                 quantize_dev(ahead, 0)
-            for job in second.get(unit, []):
-                passes(*job)
-            exponentiate(unit, 2, 4)
-            for f in stores_end.get(unit, []):
-                store_flow(on_act, 0, f)
-            if unit == 1:
-                group_elast(on_act, 0, 1, half_bank, BANK)
-            if unit == 2:
-                group_elast(on_act, 1, 1, 0, BANK)
-            if unit == 3:
-                quantize_elast(0, 1)
-                quantize_elast(1, 1)
-            if 1 < unit < GROUPS - 1:
-                scale_base(unit - 1, POOL_SHARE, BANK)
-            elif unit > 1:
-                scale_base(unit - 1, half_bank, BANK)
-                scale_base(unit - 1, POOL_SHARE, half_bank)
-            if ahead < GROUPS:
+            for passes in after_unit[unit]:
+                second_product(*passes)
+            exponentiate(unit, 2, PACK)
+            for f in stores.get(unit, []):
+                store_flow(on_scalar, 0, f)
+            if unit == last_turn:
+                group_elast(on_scalar, 1, 1, 0, BANK)
+                scale_base(nc.vector, RUN, before, POOL_SHARE, BANK)
                 quantize_dev(ahead, 1)
+            else:
+                if unit == last_of_half:
+                    quantize_elast(0, 1)
+                    quantize_elast(1, 1)
+                scale_base(nc.vector, RUN, before, HALF_BANK, BANK)
+                scale_base(nc.vector, RUN, before, POOL_SHARE, HALF_BANK)
             if ahead < UNITS:
                 for t in range(len(Y_BANKS)):
-                    respond(ahead, t)
-            for job in second_late.get(unit, []):
-                passes(*job)
-            if unit < GROUPS - 1:
-                quantize_load(unit - 1)
+                    first_product(ahead, t)
+            for passes in after_next.get(unit, []):
+                second_product(*passes)
+            if unit == last_turn:
+                quantize_load(before, 0, BANK)
             else:
-                quantize_load(unit - 1, half_bank, BANK)
-                quantize_load(unit - 1, 0, half_bank)
+                quantize_load(before, HALF_BANK, BANK)
+                quantize_load(before, 0, HALF_BANK)
 
-        passes(1, range(5, 8), [0, 1], [Y_BANKS[(PACK * last + t + 2) % len(Y_BANKS)] for t in range(1, PACK)])
-        passes(1, range(LINE_TILES), [2])
-        for step in (scale_base, quantize_load):
-            step(last, 0, half_bank)
-            step(last, half_bank, BANK)
+        second_product(1, range(5, LINE_TILES), [0, 1], [y_bank(LAST, t) for t in range(1, PACK)])
+        second_product(1, range(LINE_TILES), [2])
+        scale_base(nc.vector, RUN, LAST, 0, HALF_BANK)
+        scale_base(nc.vector, RUN, LAST, HALF_BANK, BANK)
+        quantize_load(LAST, 0, HALF_BANK)
+        quantize_load(LAST, HALF_BANK, BANK)
         for f in range(LINE_TILES):
-            flow_pass(1, f, 3)
-            store_flow(on_vec if f % 2 == 0 else on_act, 1, f)
+            second_product(1, [f], [GROUPS - 1])
+            store_flow(on_vector if f % 2 == 0 else on_scalar, 1, f)

from contextlib import ExitStack

import concourse.mybir as mybir
from concourse.masks import make_identity

NODES, PERIODS, LINES = 2048, 1024, 1024
FLOPS = 2 * NODES * PERIODS * PERIODS + 2 * NODES * LINES * PERIODS

F32 = mybir.dt.float32
BF16 = mybir.dt.bfloat16
U32 = mybir.dt.uint32
I32 = mybir.dt.int32
U8 = mybir.dt.uint8
FP8X4 = mybir.dt.float8_e4m3fn_x4
FP4X4 = mybir.dt.float4_e2m1fn_x4
ADD = mybir.AluOpType.add
MULT = mybir.AluOpType.mult
EXP = mybir.ActivationFunctionType.Exp

P = 128
PACK = 4
K_PASS = P * PACK
BANK = 512
HALF_BANK = BANK // 2
GROUPS = NODES // K_PASS
J_PASSES = PERIODS // K_PASS
LINE_TILES = LINES // P
UNITS = (PERIODS // BANK) * GROUPS
LAST = UNITS - 1

RUN = 4
POOL_RUN = 2
HEAD_SPLIT = 352
POOL_SHARE = 176

Y_BANKS = (0, 1, 2)
TURN_BANKS = (3, 4)
FLOW_BANKS = (5, 6, 7) + TURN_BANKS


def tile_cross_period_demand_flows_s13_kernel(tc, dev, elast, shift, base, ptdf_words, ptdf_scales, out):
    nc = tc.nc
    with ExitStack() as ctx:
        keep = ctx.enter_context(tc.tile_pool(name="keep", bufs=1))
        work = ctx.enter_context(tc.tile_pool(name="work", bufs=3))
        psum = ctx.enter_context(tc.psum_pool(name="psum", bufs=1))
        ctx.enter_context(tc.manual_schedule())

        def bank(b, name):
            return psum.tile([P, BANK], F32, name=name, tag="bank%d" % b)

        def y_bank(unit, t):
            return Y_BANKS[(PACK * unit + t - 1) % len(Y_BANKS)]

        def periods_of(half):
            return slice(half * BANK, (half + 1) * BANK)

        def in_runs(slots_first, run):
            return slots_first.rearrange("p t (c i) -> p c t i", i=run)

        def grouped_in_runs(grouped, run):
            return grouped.rearrange("p (c i) t -> p c t i", i=run)

        def mx_tiles(name, width):
            codes = keep.tile([P, width], U32, name=name + "_codes", align_bytes=64)
            scales = keep.tile([P, width], U8, name=name + "_scales", align_bytes=64)
            return codes, scales

        dev_rows = dev.rearrange("(g p t) j -> g p t j", p=P, t=PACK)
        base_rows = base.rearrange("(g p t) h -> g p t h", p=P, t=PACK)
        elast_rows = elast.rearrange("(c p t) h -> c p t h", p=P, t=PACK)
        dev_raw, elast_raw, base_raw, w_codes = {}, {}, {}, {}

        def load_dev(g, t0, t1):
            raw = keep.tile([P, t1 - t0, PERIODS], BF16, name="dev_%d_%d" % (g, t0))
            nc.sync.dma_start(out=raw[:], in_=dev_rows[g, :, t0:t1, :])
            for t in range(t0, t1):
                dev_raw[g, t] = raw[:, t - t0, :]

        def load_elast(c, half):
            raw = keep.tile([P, PACK, BANK], BF16, name="elast_%d_%d" % (c, half))
            nc.sync.dma_start(out=raw[:], in_=elast_rows[c, :, :, periods_of(half)])
            elast_raw[c, half] = raw

        def load_base(unit):
            half, g = divmod(unit, GROUPS)
            raw = keep.tile([P, PACK, BANK], BF16, name="base_%d" % unit)
            nc.sync.dma_start(out=raw[:], in_=base_rows[g, :, :, periods_of(half)])
            base_raw[unit] = raw

        def load_w_codes(g0, g1):
            codes = keep.tile([P, g1 - g0, 2 * LINES], U8, name="w_codes_%d" % g0, align_bytes=64)
            nc.sync.dma_start(out=codes[:].bitcast(I32), in_=ptdf_words[g0:g1].rearrange("g p n -> p g n").bitcast(I32))
            for g in range(g0, g1):
                w_codes[g] = codes[:, g - g0, :]

        w_scales = keep.tile([P, GROUPS, LINES], U8, name="w_scales", align_bytes=64)

        def load_w_scales():
            for q in range(P // 32):
                nc.sync.dma_start(
                    out=w_scales[32 * q : 32 * q + 4].bitcast(I32),
                    in_=ptdf_scales[:, 4 * q : 4 * q + 4, :].rearrange("g r n -> r g n").bitcast(I32),
                )

        ident = keep.tile([P, P], F32, name="ident")
        make_identity(nc, ident[:])
        shift_per_part = PERIODS // P
        shift_raw = keep.tile([P, shift_per_part], BF16, name="shift_raw")
        nc.scalar.dma_start(out=shift_raw[:], in_=shift.rearrange("(p c) -> p c", p=P))
        nc.vector.memset(w_scales[:].rearrange("p g n -> p (g n)").bitcast(I32), 0)

        load_elast(0, 0)
        load_dev(0, 0, 2)
        load_elast(1, 0)
        load_dev(0, 2, PACK)
        load_dev(1, 0, 2)
        load_base(0)
        load_dev(1, 2, PACK)
        load_dev(2, 0, PACK)
        load_elast(0, 1)
        load_base(1)
        load_dev(3, 0, PACK)
        load_w_scales()
        load_w_codes(0, 2)
        load_elast(1, 1)
        load_base(2)
        load_w_codes(2, GROUPS)
        for later_unit in range(3, UNITS):
            load_base(later_unit)

        shift_all = keep.tile([P, PERIODS], BF16, name="shift_all")

        def spread_shift():
            words = shift_per_part // 2
            pairs = shift_raw[:].bitcast(F32)
            spread = bank(Y_BANKS[0], "spread")
            for c in range(words):
                nc.tensor.transpose(spread[:, c * P : (c + 1) * P], pairs[:, c : c + 1].to_broadcast([P, P]), ident[:])
            nc.scalar.copy(
                out=shift_all[:].bitcast(F32).rearrange("p (k c) -> p k c", c=words),
                in_=spread[:].rearrange("p (c k) -> p k c", c=words),
            )

        elast_grouped, elast_q = {}, {}

        def group_elast(copy, c, half, h0, h1):
            if (c, half) not in elast_grouped:
                elast_grouped[c, half] = work.tile(
                    [P, BANK, PACK], BF16, name="eg_%d_%d" % (c, half), tag="eg", bufs=J_PASSES, align_bytes=64
                )
            copy(
                out=grouped_in_runs(elast_grouped[c, half][:, h0:h1, :], RUN),
                in_=in_runs(elast_raw[c, half][:, :, h0:h1], RUN),
            )

        def quantize_elast(c, half):
            codes, scales = mx_tiles("eq_%d_%d" % (c, half), BANK)
            nc.vector.quantize_mx(
                out=codes[:].bitcast(FP8X4),
                scales=scales[:],
                in_=elast_grouped[c, half][:].rearrange("p h t -> p (h t)"),
            )
            elast_q[c, half] = codes, scales

        dev_grouped, dev_q = {}, {}

        def turn_dev(g, t):
            pair, member = divmod(t, 2)
            if member == 0:
                dev_grouped[g, pair] = work.tile(
                    [P, 2, J_PASSES, P * PACK], BF16, name="dg_%d_%d" % (g, pair), tag="dg", align_bytes=64
                )
            words = dev_raw[g, t].bitcast(F32)
            pass_words = K_PASS // 2
            turned = bank(TURN_BANKS[member], "turned_%d_%d" % (g, t))
            for c in range(J_PASSES):
                for u in range(2):
                    nc.tensor.transpose(
                        turned[:, (2 * c + u) * P : (2 * c + u + 1) * P],
                        words[:, pass_words * c + u : pass_words * (c + 1) : 2],
                        ident[:],
                    )
            nc.scalar.copy(
                out=dev_grouped[g, pair][:, member].bitcast(F32).rearrange("p c (n u) -> p c n u", u=2),
                in_=turned[:].rearrange("p (c u n) -> p c n u", c=J_PASSES, u=2),
            )

        def turn_dev_pair(g, pair):
            turn_dev(g, 2 * pair)
            turn_dev(g, 2 * pair + 1)

        def quantize_dev(g, pair):
            codes, scales = mx_tiles("dq_%d_%d" % (g, pair), 2 * J_PASSES * P)
            nc.vector.quantize_mx(
                out=codes[:].bitcast(FP8X4),
                scales=scales[:],
                in_=dev_grouped[g, pair][:].rearrange("p s c n -> p (s c n)"),
            )
            dev_q[g, pair] = codes, scales

        y_sums, response = {}, {}

        def first_product(unit, t):
            half, g = divmod(unit, GROUPS)
            pair, member = divmod(t, 2)
            y_sums[unit, t] = bank(y_bank(unit, t), "y_%d_%d" % (unit, t))
            d_codes, d_scales = dev_q[g, pair]
            for c in range(J_PASSES):
                nodes = slice((J_PASSES * member + c) * P, (J_PASSES * member + c + 1) * P)
                e_codes, e_scales = elast_q[c, half]
                nc.tensor.matmul_mx(
                    out=y_sums[unit, t][:],
                    lhsT=d_codes[:, nodes].bitcast(FP8X4),
                    lhsT_scale=d_scales[:, nodes],
                    rhs=e_codes[:].bitcast(FP8X4),
                    rhs_scale=e_scales[:],
                    start=(c == 0),
                    stop=(c == J_PASSES - 1),
                )

        def add_shift(unit, t):
            if t == 0:
                response[unit] = work.tile([P, PACK, BANK], F32, name="resp_%d" % unit, tag="resp")
            nc.vector.tensor_tensor(
                out=response[unit][:, t, :], in0=y_sums[unit, t][:], in1=shift_all[:, periods_of(unit // GROUPS)], op=ADD
            )

        def exponentiate(unit, t0, t1):
            part = response[unit][:, t0:t1, :]
            nc.scalar.activation(out=part, in_=part, func=EXP)

        load_grouped, load_q = {}, {}

        def scale_base(engine, run, unit, h0, h1):
            if unit not in load_grouped:
                load_grouped[unit] = work.tile(
                    [P, BANK, PACK], BF16, name="lg_%d" % unit, tag="lg", bufs=1, align_bytes=64
                )
            engine.tensor_tensor(
                out=grouped_in_runs(load_grouped[unit][:, h0:h1, :], run),
                in0=in_runs(response[unit][:, :, h0:h1], run),
                in1=in_runs(base_raw[unit][:, :, h0:h1], run),
                op=MULT,
            )

        def quantize_load(unit, h0, h1):
            if unit not in load_q:
                load_q[unit] = mx_tiles("lq_%d" % unit, BANK)
            codes, scales = load_q[unit]
            nc.vector.quantize_mx(
                out=codes[:, h0:h1].bitcast(FP8X4),
                scales=scales[:, h0:h1],
                in_=load_grouped[unit][:, h0:h1, :].rearrange("p h t -> p (h t)"),
            )

        flows = {}

        def second_product(half, line_tiles, groups, banks=()):
            for n, f in enumerate(line_tiles):
                for g in groups:
                    if g == 0:
                        flows[half, f] = bank(banks[n], "flow_%d_%d" % (half, f))
                    l_codes, l_scales = load_q[half * GROUPS + g]
                    nc.tensor.matmul_mx(
                        out=flows[half, f][:],
                        lhsT=w_codes[g][:, 2 * P * f : 2 * P * (f + 1)].bitcast(FP4X4),
                        lhsT_scale=w_scales[:, g, P * f : P * (f + 1)],
                        rhs=l_codes[:].bitcast(FP8X4),
                        rhs_scale=l_scales[:],
                        start=(g == 0),
                        stop=(g == GROUPS - 1),
                    )

        def store_flow(copy, half, f):
            done = work.tile([P, BANK], F32, name="done_%d_%d" % (half, f), tag="done", bufs=LINE_TILES)
            copy(out=done[:], in_=flows[half, f][:])
            nc.sync.dma_start(out=out[P * f : P * (f + 1), periods_of(half)], in_=done[:])

        on_scalar, on_vector = nc.scalar.copy, nc.vector.tensor_copy

        spread_shift()
        group_elast(on_scalar, 0, 0, HEAD_SPLIT, BANK)
        group_elast(on_vector, 0, 0, 0, HEAD_SPLIT)
        turn_dev_pair(0, 0)
        quantize_elast(0, 0)
        group_elast(on_vector, 1, 0, 0, BANK)
        quantize_dev(0, 0)
        quantize_elast(1, 0)
        turn_dev_pair(0, 1)

        first_product(0, 0)
        first_product(0, 1)
        add_shift(0, 0)
        exponentiate(0, 0, 1)
        quantize_dev(0, 1)
        add_shift(0, 1)
        turn_dev_pair(1, 0)
        exponentiate(0, 1, 2)
        quantize_dev(1, 0)
        first_product(0, 2)
        first_product(0, 3)
        add_shift(0, 2)
        add_shift(0, 3)
        turn_dev_pair(1, 1)
        first_product(1, 0)
        first_product(1, 1)
        exponentiate(0, 2, PACK)
        group_elast(on_scalar, 0, 1, 0, HALF_BANK)

        add_shift(1, 0)
        quantize_dev(1, 1)
        turn_dev_pair(2, 0)
        first_product(1, 2)
        first_product(1, 3)
        add_shift(1, 1)
        scale_base(nc.vector, RUN, 0, 0, BANK)
        quantize_dev(2, 0)
        exponentiate(1, 0, 2)
        add_shift(1, 2)
        add_shift(1, 3)
        turn_dev_pair(2, 1)
        exponentiate(1, 2, PACK)
        group_elast(on_scalar, 0, 1, HALF_BANK, BANK)
        quantize_dev(2, 1)
        for t in range(len(Y_BANKS)):
            first_product(2, t)
        quantize_load(0, 0, BANK)

        after_unit = {
            2: [(0, range(3), [0], FLOW_BANKS)],
            3: [(0, range(3), [1]), (0, range(3, 5), [0, 1], FLOW_BANKS[3:])],
            4: [(0, range(5), [2])],
            5: [(0, range(5), [3])],
            6: [(0, [6, 7], range(GROUPS), FLOW_BANKS[1:]), (1, [0], [0], FLOW_BANKS[3:])],
            7: [(1, range(2), [1]), (1, range(2, 5), [0, 1], FLOW_BANKS)],
        }
        after_next = {
            5: [(0, [5], range(GROUPS), FLOW_BANKS)],
            6: [(1, [1], [0], FLOW_BANKS[4:])],
        }
        stores = {5: range(4), 6: range(4, LINE_TILES)}
        last_turn = GROUPS - 2
        last_of_half = GROUPS - 1

        for unit in range(2, UNITS):
            before, ahead = unit - 1, unit + 1
            scale_base(nc.gpsimd, POOL_RUN, before, 0, POOL_SHARE)
            add_shift(unit, 0)
            if unit == last_turn:
                turn_dev_pair(ahead, 0)
            first_product(unit, PACK - 1)
            add_shift(unit, 1)
            exponentiate(unit, 0, 2)
            add_shift(unit, 2)
            add_shift(unit, 3)
            if unit == last_turn:
                turn_dev_pair(ahead, 1)
                quantize_dev(ahead, 0)
            for passes in after_unit[unit]:
                second_product(*passes)
            exponentiate(unit, 2, PACK)
            for f in stores.get(unit, []):
                store_flow(on_scalar, 0, f)
            if unit == last_turn:
                group_elast(on_scalar, 1, 1, 0, BANK)
                scale_base(nc.vector, RUN, before, POOL_SHARE, BANK)
                quantize_dev(ahead, 1)
            else:
                if unit == last_of_half:
                    quantize_elast(0, 1)
                    quantize_elast(1, 1)
                scale_base(nc.vector, RUN, before, HALF_BANK, BANK)
                scale_base(nc.vector, RUN, before, POOL_SHARE, HALF_BANK)
            if ahead < UNITS:
                for t in range(len(Y_BANKS)):
                    first_product(ahead, t)
            for passes in after_next.get(unit, []):
                second_product(*passes)
            if unit == last_turn:
                quantize_load(before, 0, BANK)
            else:
                quantize_load(before, HALF_BANK, BANK)
                quantize_load(before, 0, HALF_BANK)

        second_product(1, range(5, LINE_TILES), [0, 1], [y_bank(LAST, t) for t in range(1, PACK)])
        second_product(1, range(LINE_TILES), [2])
        scale_base(nc.vector, RUN, LAST, 0, HALF_BANK)
        scale_base(nc.vector, RUN, LAST, HALF_BANK, BANK)
        quantize_load(LAST, 0, HALF_BANK)
        quantize_load(LAST, HALF_BANK, BANK)
        for f in range(LINE_TILES):
            second_product(1, [f], [GROUPS - 1])
            store_flow(on_vector if f % 2 == 0 else on_scalar, 1, f)
